import numpy as np
import ml_dtypes


def mxq(x, axis, fmt="e4m3"):
    dtype, down = {"e4m3": (ml_dtypes.float8_e4m3fn, 7), "e5m2": (ml_dtypes.float8_e5m2, 14)}[fmt]
    v = np.moveaxis(np.asarray(x, np.float32).astype(ml_dtypes.bfloat16).astype(np.float64), axis, -1)
    blocks = v.reshape(v.shape[:-1] + (-1, 32))
    amax = np.abs(blocks).max(-1, keepdims=True)
    byte = np.maximum(np.where(amax > 0, np.frexp(amax)[1] - 1 + 127, 0) - down, 1)
    scale = np.exp2(byte - 127.0)
    codes = (blocks / scale).astype(np.float32).astype(dtype).astype(np.float64)
    return np.moveaxis((codes * scale).reshape(v.shape), -1, axis)


WIDE = False


def mx_kscale(k):
    if not WIDE:
        return np.ones(k)
    levels = np.array([10, -10, 5, -5, 0])
    if k % 512:
        return np.exp2(np.random.permutation(np.resize(levels, k // 32))).repeat(32)
    a = np.empty((k // 512, 16))
    for p in range(k // 512):
        a[p, :8] = np.random.permutation(np.resize(levels, 8))
        for g in range(8):
            far = levels[np.abs(levels - a[p, g]) >= 10]
            a[p, g + 8] = far[np.random.randint(len(far))]
    return np.exp2(a.ravel()).repeat(32)


def f64(x):
    return np.asarray(x).astype(np.float64)


def striped(idx):
    return np.tile(idx.reshape(-1, 16).T, (8, 1)).astype(np.uint16)


def unstriped(offs):
    return offs[:16].T.reshape(-1).astype(np.int64)


E2M1 = np.array([0.0, 0.5, 1.0, 1.5, 2.0, 3.0, 4.0, 6.0, -0.0, -0.5, -1.0, -1.5, -2.0, -3.0, -4.0, -6.0])


def pack_weight(w, fmt):
    k, n = w.shape
    w = f64(np.asarray(w, np.float32).astype(ml_dtypes.bfloat16)).reshape(k // 32, 32, n)
    amax = np.abs(w).max(1)
    if fmt == "e4m3":
        byte = np.frexp(amax)[1] - 1 + 127 - 7
    else:
        mant, ex = np.frexp(amax / 6.0)
        byte = np.where(mant > 0.5, ex, ex - 1) + 127
    byte = np.clip(np.where(amax > 0, byte, 1), 1, 254)
    scaled = (w * np.exp2(127.0 - byte)[:, None, :]).reshape(k, n).astype(np.float32)
    by_word = np.ascontiguousarray(scaled.reshape(k // 512, 128, 4, n).transpose(0, 1, 3, 2))
    if fmt == "e4m3":
        words = by_word.astype(ml_dtypes.float8_e4m3fn).view(np.uint8)
    else:
        c = by_word.astype(ml_dtypes.float4_e2m1fn).view(np.uint8) & 0xF
        words = (c[..., 0::2] | (c[..., 1::2] << 4)).reshape(k // 512, 128, 2 * n)
    return np.ascontiguousarray(words), np.ascontiguousarray(byte.astype(np.uint8).reshape(k // 512, 16, n))


def unpack_weight(words, scales, fmt):
    g, _, n = scales.shape
    words = np.ascontiguousarray(words).reshape(g, 128, n, -1)
    if fmt == "e4m3":
        vals = words.view(ml_dtypes.float8_e4m3fn).astype(np.float64)
    else:
        nib = np.empty((g, 128, n, 4), np.uint8)
        nib[..., 0::2] = words & 0xF
        nib[..., 1::2] = words >> 4
        vals = E2M1[nib]
    vals = vals * np.repeat(np.exp2(scales.astype(np.float64) - 127.0), 8, axis=1)[..., None]
    return vals.transpose(0, 1, 3, 2).reshape(g * 512, n)


def gelu(v):
    return 0.5 * v * (1.0 + np.tanh(np.sqrt(2.0 / np.pi) * (v + 0.044715 * v**3)))


def bf(x):
    return np.asarray(x, np.float32).astype(ml_dtypes.bfloat16)


def planes(Y):
    n, m = Y.shape
    b = f64(bf(Y)).reshape(n // 32, 32, m)
    amax = np.abs(b).max(1)
    byte = np.clip(np.where(amax > 0, np.frexp(amax)[1] - 1 + 127 - 7, 1), 1, 254)
    codes = (b * np.exp2(127.0 - byte)[:, None, :]).reshape(n, m).astype(np.float32).astype(ml_dtypes.float8_e4m3fn).view(np.uint8)
    words = codes.reshape(n // 512, 128, 4, m).transpose(0, 1, 3, 2)
    return np.ascontiguousarray(words), np.ascontiguousarray(byte.astype(np.uint8).reshape(n // 512, 16, m))


K, H, N, T, S, T2, P = 1024, 512, 512, 2048, 1024, 2048, 1024

def setup_inputs():
    n = np.random.standard_normal
    s = mx_kscale(K)[:, None]
    u = mx_kscale(H)[:, None]
    spread = np.exp(0.8 * n(N))
    tab_words, tab_scales = pack_weight(n((K, T)) * s, "e4m3")
    w2_words, w2_scales = pack_weight(0.55 * n((K, H)) / np.sqrt(K) / s, "e2m1")
    w4_words, w4_scales = pack_weight(3.0 * n((H, N)) / np.sqrt(H) / u * spread, "e4m3")
    return {
        "tab_words": tab_words, "tab_scales": tab_scales,
        "offs": striped(np.random.permutation(T)[:S]),
        "offs2": striped(np.random.permutation(T2)[:S]),
        "offs3": striped(np.random.permutation(T2)[:P]),
        "w1": (0.55 * n((K, H)) / np.sqrt(K) / s).astype(np.float32),
        "w2_words": w2_words, "w2_scales": w2_scales,
        "w3": (0.65 * n((K, H)) / np.sqrt(K) / s).astype(np.float32),
        "page0": (0.8 * n((H, T2))).astype(np.float32),
        "wgs": np.exp(0.3 * n((128, S))).astype(np.float32),
        "gain": (np.sign(n(H)) * np.random.uniform(2.5, 5.0, H) * u[:, 0]).astype(np.float32),
        "w4_words": w4_words, "w4_scales": w4_scales,
        "w5": (3.0 * n((H, N)) / np.sqrt(H) / u * spread).astype(np.float32),
    }

def reference(tab_words, tab_scales, offs, offs2, offs3, w1, w2_words, w2_scales, w3, page0, wgs, gain, w4_words, w4_scales, w5):
    v = unpack_weight(tab_words, tab_scales, "e4m3")[:, unstriped(offs)]
    w2 = unpack_weight(w2_words, w2_scales, "e2m1")
    w4 = unpack_weight(w4_words, w4_scales, "e4m3")
    first = mxq(f64(w1), 0, "e4m3").T @ v
    second = w2.T @ v
    third = mxq(f64(w3), 0, "e4m3").T @ v
    h = first * second + third
    page = f64(page0).copy()
    page[:, unstriped(offs2)] = np.tile(f64(wgs), (H // 128, 1)) * h
    top = page.max(axis=1)
    a = np.exp(page[:, unstriped(offs3)] - top[:, None])
    z = mxq(f64(gain)[:, None] * a, 0, "e4m3")
    y = (w4.T @ z) + np.abs(mxq(f64(w5), 0, "e4m3").T @ z)
    words, scales = planes(y)
    return y, words, scales

@@ -1,0 +1,320 @@
+from contextlib import ExitStack
+
+import concourse.mybir as mybir
+
+F32 = mybir.dt.float32
+BF16 = mybir.dt.bfloat16
+I32 = mybir.dt.int32
+U32 = mybir.dt.uint32
+U16 = mybir.dt.uint16
+U8 = mybir.dt.uint8
+FP8X4 = mybir.dt.float8_e4m3fn_x4
+FP4X4 = mybir.dt.float4_e2m1fn_x4
+ALU = mybir.AluOpType
+ACT = mybir.ActivationFunctionType
+AXIS = mybir.AxisListType
+
+K, H, N, T, S, T2, M = 1024, 512, 512, 2048, 1024, 2048, 1024
+FLOPS = 2 * K * H * S * 3 + 2 * H * N * M * 2
+
+P = 128
+PACK = 4
+PASSES = K // (P * PACK)
+BLOCKS = H // P
+HALF = 512
+HALVES = S // HALF
+LIST_COLS = HALF // 16
+CHUNK = 256
+QUADS = 4
+
+
+def tile_list_carousel_greasing_log_kernel(
+    tc, tab_words, tab_scales, offs, offs2, offs3, w1, w2_words, w2_scales, w3, page0, wgs, gain,
+    w4_words, w4_scales, w5, out_0, out_1, out_2,
+):
+    nc = tc.nc
+    with ExitStack() as ctx:
+        lists = ctx.enter_context(tc.tile_pool(name="lists", bufs=1))
+        keep = ctx.enter_context(tc.tile_pool(name="keep", bufs=1))
+        ring = ctx.enter_context(tc.tile_pool(name="ring", bufs=2))
+        psum = ctx.enter_context(tc.psum_pool(name="psum", bufs=2))
+
+        def kept(shape, dtype, name, tag=""):
+            return keep.tile(shape, dtype, name=name, tag=tag or name, align_bytes=64)
+
+        idx1 = lists.tile([P, S // 16], U16, name="idx1")
+        idx2 = lists.tile([P, S // 16], U16, name="idx2")
+        idx3 = lists.tile([P, M // 16], U16, name="idx3")
+
+        tab_s = kept([P, T], U8, "tab_s")
+        got_s1 = kept([P, S], U8, "got_s1")
+        w2_s = kept([P, PASSES, H], U8, "w2_s")
+        w4_s_raw = kept([P, N], U8, "w4_s_raw")
+        nc.vector.memset(tab_s[:].bitcast(I32), 0)
+        nc.vector.memset(w2_s[:].rearrange("p a c -> p (a c)").bitcast(I32), 0)
+        nc.vector.memset(got_s1[:].bitcast(I32), 0)
+        nc.vector.memset(w4_s_raw[:].bitcast(I32), 0)
+
+        tab_w = [kept([P, T], I32, "tab_w%d" % a) for a in range(PASSES)]
+
+        def load_tab(a):
+            nc.sync.dma_start(out=tab_w[a][:], in_=tab_words[a].rearrange("p t i -> p (t i)").bitcast(I32))
+
+        nc.sync.dma_start(idx1[:], offs)
+        load_tab(0)
+        for q in range(QUADS):
+            nc.sync.dma_start(
+                out=tab_s[32 * q : 32 * q + 4 * PASSES, :].bitcast(I32),
+                in_=tab_scales[:, 4 * q : 4 * q + 4, :].bitcast(I32),
+            )
+        for q in range(QUADS):
+            nc.gpsimd.dma_start(
+                out=w2_s[32 * q : 32 * q + 4, :, :].bitcast(I32),
+                in_=w2_scales[:, 4 * q : 4 * q + 4, :].rearrange("a r c -> r a c").bitcast(I32),
+            )
+
+        weights = (w1, w3)
+        spans = ((0, 1), (1, 2), (2, 4))
+        raws = {}
+
+        def load_weights(span):
+            lo, hi = span
+            for w in range(2):
+                raw = kept([P, PASSES, PACK, P * (hi - lo)], F32, "raw%d_%d" % (w, lo))
+                for a in range(PASSES):
+                    rows = weights[w][512 * a : 512 * (a + 1), :].rearrange("(p j) c -> p j c", j=PACK)
+                    nc.sync.dma_start(out=raw[:, a, :, :], in_=rows[:, :, P * lo : P * hi])
+                for b in range(lo, hi):
+                    raws[w, b] = raw[:, :, :, P * (b - lo) : P * (b - lo + 1)]
+
+        w2_w = kept([P, PASSES, 2 * H], U8, "w2_w")
+        wgs_t = kept([P, S], F32, "wgs_t")
+        pages = [kept([P, T2], F32, "page%d" % b) for b in range(BLOCKS)]
+        gain_t = kept([P, BLOCKS], F32, "gain_t")
+        w4_raw = kept([P, N], I32, "w4_raw")
+        w5_raw = kept([P, PACK, N], F32, "w5_raw")
+
+        def load_page(b):
+            nc.sync.dma_start(out=pages[b][:], in_=page0[P * b : P * (b + 1), :])
+
+        load_weights(spans[0])
+        load_tab(1)
+
+        got_w = [[kept([P, HALF], U32, "got_w%d_%d" % (a, h)) for h in range(HALVES)] for a in range(PASSES)]
+        got_s = kept([P, S], U8, "got_s")
+
+        def half_of(idx, h):
+            return idx[:, LIST_COLS * h : LIST_COLS * (h + 1)]
+
+        def gather_words(a, h):
+            nc.vector.tensor_copy(got_w[a][h][:], tab_w[a][:].bitcast(U32).indirect(half_of(idx1, h)))
+
+        w_codes = {}
+        w_scales = {}
+
+        def quantise_weight(w, b):
+            raw = raws[w, b]
+            rounded = kept([P, PASSES, P, PACK], BF16, "w_rounded%d_%d" % (w, b), tag="w_rounded%d_%d" % (w, b % 2))
+            nc.scalar.copy(
+                out=rounded[:].rearrange("p a (c i) j -> p a c j i", i=4),
+                in_=raw.rearrange("p a j (c i) -> p a c j i", i=4),
+            )
+            w_codes[w, b] = kept([P, PASSES, P], U32, "w_codes%d_%d" % (w, b))
+            w_scales[w, b] = kept([P, PASSES, P], U8, "w_scales%d_%d" % (w, b))
+            nc.vector.quantize_mx(
+                out=w_codes[w, b][:].rearrange("p a c -> p (a c)").bitcast(FP8X4),
+                scales=w_scales[w, b][:].rearrange("p a c -> p (a c)"),
+                in_=rounded[:].rearrange("p a c j -> p (a c j)"),
+            )
+
+        gather_words(0, 0)
+        nc.vector.tensor_copy(got_s[:], tab_s[:].indirect(idx1[:]))
+        for q in range(QUADS):
+            nc.sync.dma_start(
+                out=got_s1[32 * q : 32 * q + 4, :].bitcast(I32),
+                in_=got_s[32 * q + 4 : 32 * q + 8, :].bitcast(I32),
+            )
+        quantise_weight(0, 0)
+        quantise_weight(1, 0)
+        gather_words(1, 0)
+        gather_words(0, 1)
+        gather_words(1, 1)
+
+        nc.sync.dma_start(out=w2_w[:].bitcast(I32), in_=w2_words.rearrange("a p c -> p a c").bitcast(I32))
+        nc.sync.dma_start(idx2[:], offs2)
+        nc.sync.dma_start(out=wgs_t[:], in_=wgs)
+        load_page(0)
+        load_weights(spans[1])
+        load_weights(spans[2])
+        load_page(1)
+        nc.sync.dma_start(idx3[:], offs3)
+        with nc.allow_non_contiguous_dma(reason="one gain for each row of a block, rows on the partitions"):
+            nc.sync.dma_start(out=gain_t[:], in_=gain.rearrange("(b p) -> p b", p=P))
+        load_page(2)
+        load_page(3)
+        nc.sync.dma_start(out=w5_raw[:], in_=w5.rearrange("(p j) c -> p j c", j=PACK))
+        nc.sync.dma_start(out=w4_raw[:], in_=w4_words[0].rearrange("p c i -> p (c i)").bitcast(I32))
+        for q in range(QUADS):
+            nc.sync.dma_start(
+                out=w4_s_raw[32 * q : 32 * q + 4, :].bitcast(I32),
+                in_=w4_scales[0, 4 * q : 4 * q + 4, :].bitcast(I32),
+            )
+
+        def products(b, h):
+            cols = slice(HALF * h, HALF * (h + 1))
+            first = psum.tile([P, HALF], F32, name="bank_a")
+            second = psum.tile([P, HALF], F32, name="bank_b")
+            third = psum.tile([P, HALF], F32, name="bank_c")
+            for w, bank in ((0, first), (1, third)):
+                for a in range(PASSES):
+                    nc.tensor.matmul_mx(
+                        out=bank[:],
+                        lhsT=w_codes[w, b][:, a, :].bitcast(FP8X4),
+                        lhsT_scale=w_scales[w, b][:, a, :],
+                        rhs=got_w[a][h][:].bitcast(FP8X4),
+                        rhs_scale=got_s[4 * a : P, cols],
+                        start=(a == 0),
+                        stop=(a == PASSES - 1),
+                    )
+            for a in range(PASSES):
+                nc.tensor.matmul_mx(
+                    out=second[:],
+                    lhsT=w2_w[:, a, 2 * P * b : 2 * P * (b + 1)].bitcast(FP4X4),
+                    lhsT_scale=w2_s[:, a, P * b : P * (b + 1)],
+                    rhs=got_w[a][h][:].bitcast(FP8X4),
+                    rhs_scale=(got_s, got_s1)[a][:, cols],
+                    start=(a == 0),
+                    stop=(a == PASSES - 1),
+                )
+            first_sb = ring.tile([P, HALF], F32, name="first_sb")
+            nc.scalar.copy(out=first_sb[:], in_=first[:])
+            prod = kept([P, HALF], F32, "prod%d_%d" % (b, h), tag="prod%d_%d" % (b % 2, h))
+            nc.vector.tensor_tensor(prod[:], second[:], first_sb[:], ALU.mult)
+            return prod, third
+
+        def add_third(h_cols, prod, third):
+            nc.vector.tensor_tensor(h_cols, third[:], prod[:], ALU.add)
+
+        z_rows = [kept([P, PACK, HALF], BF16, "z_rows%d" % h) for h in range(HALVES)]
+
+        def look(b, neg_top):
+            nc.vector.tensor_reduce(neg_top, pages[b][:], AXIS.X, ALU.max, negate=True)
+            for h in range(HALVES):
+                a_sb = ring.tile([P, HALF], F32, name="a_sb")
+                nc.scalar.activation(
+                    out=a_sb[:], in_=pages[b][:].indirect(half_of(idx3, h)), func=ACT.Exp, bias=neg_top
+                )
+                z_sb = ring.tile([P, HALF], BF16, name="z_sb")
+                if b == BLOCKS - 1:
+                    nc.vector.tensor_scalar(z_sb[:], a_sb[:], gain_t[:, b : b + 1], None, ALU.mult)
+                else:
+                    nc.scalar.activation(out=z_sb[:], in_=a_sb[:], func=ACT.Copy, scale=gain_t[:, b : b + 1])
+                for t in range(PACK):
+                    nc.sync.dma_start(out=z_rows[h][32 * b : 32 * (b + 1), t, :], in_=z_sb[t:P:PACK, :])
+
+        parts = products(0, 0)
+        h_first = kept([P, HALF], F32, "h_first")
+        add_third(h_first[:], *parts)
+        parts = products(0, 1)
+        nc.vector.tensor_tensor(pages[0][:].indirect(half_of(idx2, 0)), h_first[:], wgs_t[:, 0:HALF], ALU.mult)
+        quantise_weight(0, 1)
+        quantise_weight(1, 1)
+        h_second = kept([P, HALF], F32, "h_second", tag="w_rounded1_1")
+        add_third(h_second[:], *parts)
+        nc.vector.tensor_tensor(pages[0][:].indirect(half_of(idx2, 1)), h_second[:], wgs_t[:, HALF:S], ALU.mult)
+        for b in range(1, BLOCKS):
+            if b + 1 < BLOCKS:
+                quantise_weight(0, b + 1)
+                quantise_weight(1, b + 1)
+            both = [products(b, h) for h in range(HALVES)]
+            h_sb = kept([P, S], F32, "h_sb%d" % b, tag="h_sb")
+            for h in range(HALVES):
+                add_third(h_sb[:, HALF * h : HALF * (h + 1)], *both[h])
+            look(b - 1, both[1][0][:, 0:1])
+            nc.vector.tensor_tensor(pages[b][:].indirect(idx2[:]), h_sb[:], wgs_t[:], ALU.mult)
+        last_top = kept([P, 1], F32, "last_top")
+        look(BLOCKS - 1, last_top[:])
+
+        w4_w = kept([P, PACK, P], I32, "w4_w")
+        w4_s = kept([P, PACK, P], U8, "w4_s", tag="wgs_t")
+        nc.scalar.copy(out=w4_w[:].bitcast(U32), in_=w4_raw[:].bitcast(U32).rearrange("p (m t) -> p t m", t=PACK))
+        nc.vector.tensor_copy(out=w4_s[:], in_=w4_s_raw[:].rearrange("p (m t) -> p t m", t=PACK))
+        w5_rounded = kept([P, PACK, P, PACK], BF16, "w5_rounded")
+        nc.scalar.copy(
+            out=w5_rounded[:].rearrange("p t m j -> p m t j"),
+            in_=w5_raw[:].rearrange("p j (m t) -> p m t j", t=PACK),
+        )
+        w5_w = kept([P, PACK, P], U32, "w5_w", tag="h_sb")
+        w5_s = kept([P, PACK, P], U8, "w5_s")
+        nc.vector.quantize_mx(
+            out=w5_w[:].rearrange("p t m -> p (t m)").bitcast(FP8X4),
+            scales=w5_s[:].rearrange("p t m -> p (t m)"),
+            in_=w5_rounded[:].rearrange("p t m j -> p (t m j)"),
+        )
+
+        y_words = kept([P, M], I32, "y_words")
+        y_scales = kept([P, M], U8, "y_scales")
+        out_rows = out_0.rearrange("(p t) m -> p t m", t=PACK)
+        out_words = out_1[0].rearrange("p m t -> p (m t)").bitcast(I32)
+
+        def quantise_z(c):
+            h, lo = divmod(CHUNK * c, HALF)
+            z_in = ring.tile([P, CHUNK, PACK], BF16, name="z_in", align_bytes=64)
+            nc.vector.tensor_copy(
+                out=z_in[:].rearrange("p (c i) t -> p c t i", i=4),
+                in_=z_rows[h][:, :, lo : lo + CHUNK].rearrange("p t (c i) -> p c t i", i=4),
+            )
+            z_w = kept([P, CHUNK], U32, "z_w%d" % c)
+            z_s = kept([P, CHUNK], U8, "z_s%d" % c)
+            nc.vector.quantize_mx(out=z_w[:].bitcast(FP8X4), scales=z_s[:], in_=z_in[:].rearrange("p m t -> p (m t)"))
+            return z_w, z_s
+
+        def second_stage(c, z_w, z_s):
+            y = kept([P, PACK, CHUNK], F32, "y%d" % c)
+            for pair in range(2):
+                plain = psum.tile([P, 2, CHUNK], F32, name=("bank_a", "bank_b")[pair])
+                other = psum.tile([P, 2, CHUNK], F32, name=("bank_c", "bank_d")[pair])
+                for codes, scales, bank in ((w5_w, w5_s, other), (w4_w, w4_s, plain)):
+                    for i in range(2):
+                        t = 2 * pair + i
+                        nc.tensor.matmul_mx(
+                            out=bank[:, i, :],
+                            lhsT=codes[:, t, :].bitcast(FP8X4),
+                            lhsT_scale=scales[:, t, :],
+                            rhs=z_w[:].bitcast(FP8X4),
+                            rhs_scale=z_s[:],
+                            start=True,
+                            stop=True,
+                        )
+                size = ring.tile([P, 2, CHUNK], F32, name="size")
+                nc.scalar.activation(out=size[:], in_=other[:], func=ACT.Abs)
+                nc.vector.tensor_tensor(y[:, 2 * pair : 2 * pair + 2, :], plain[:], size[:], ALU.add)
+            cols = slice(CHUNK * c, CHUNK * (c + 1))
+            nc.sync.dma_start(out=out_rows[:, :, cols], in_=y[:])
+            return y
+
+        def planes(c, y):
+            cols = slice(CHUNK * c, CHUNK * (c + 1))
+            y_in = ring.tile([P, CHUNK, PACK], BF16, name="y_in", align_bytes=64)
+            cast = nc.vector.tensor_copy if c == M // CHUNK - 1 else nc.scalar.copy
+            cast(
+                out=y_in[:].rearrange("p (c i) t -> p c t i", i=4),
+                in_=y[:].rearrange("p t (c i) -> p c t i", i=4),
+            )
+            nc.vector.quantize_mx(
+                out=y_words[:, cols].bitcast(FP8X4), scales=y_scales[:, cols], in_=y_in[:].rearrange("p m t -> p (m t)")
+            )
+            nc.sync.dma_start(out=out_words[:, cols], in_=y_words[:, cols])
+
+        chunks = M // CHUNK
+        zq = [quantise_z(c) for c in range(chunks)]
+        ys = []
+        for c in range(chunks):
+            ys.append(second_stage(c, *zq[c]))
+            if c > 0:
+                planes(c - 1, ys[c - 1])
+        planes(chunks - 1, ys[chunks - 1])
+        for q in range(QUADS):
+            nc.scalar.dma_start(
+                out=out_2[0, 4 * q : 4 * q + 4, :].bitcast(I32), in_=y_scales[32 * q : 32 * q + 4, :].bitcast(I32)
+            )

@@ -26,6 +26,8 @@ HALVES = S // HALF
 LIST_COLS = HALF // 16
 CHUNK = 256
 QUADS = 4
+S_WEAVES = ()
+S_CASTS = (0, 1, 2)
 
 
 def tile_list_carousel_greasing_log_kernel(
@@ -37,7 +39,7 @@ def tile_list_carousel_greasing_log_kernel(
         lists = ctx.enter_context(tc.tile_pool(name="lists", bufs=1))
         keep = ctx.enter_context(tc.tile_pool(name="keep", bufs=1))
         ring = ctx.enter_context(tc.tile_pool(name="ring", bufs=2))
-        psum = ctx.enter_context(tc.psum_pool(name="psum", bufs=2))
+        psum = ctx.enter_context(tc.psum_pool(name="psum", bufs=1))
 
         def kept(shape, dtype, name, tag=""):
             return keep.tile(shape, dtype, name=name, tag=tag or name, align_bytes=64)
@@ -74,21 +76,20 @@ def tile_list_carousel_greasing_log_kernel(
             )
 
         weights = (w1, w3)
-        spans = ((0, 1), (1, 2), (2, 4))
         raws = {}
 
-        def load_weights(span):
-            lo, hi = span
-            for w in range(2):
-                raw = kept([P, PASSES, PACK, P * (hi - lo)], F32, "raw%d_%d" % (w, lo))
-                for a in range(PASSES):
-                    rows = weights[w][512 * a : 512 * (a + 1), :].rearrange("(p j) c -> p j c", j=PACK)
-                    nc.sync.dma_start(out=raw[:, a, :, :], in_=rows[:, :, P * lo : P * hi])
-                for b in range(lo, hi):
-                    raws[w, b] = raw[:, :, :, P * (b - lo) : P * (b - lo + 1)]
+        def load_weight(w, b):
+            raws[w, b] = kept([P, PASSES, PACK, P], F32, "raw%d_%d" % (w, b))
+            for a in range(PASSES):
+                rows = weights[w][512 * a : 512 * (a + 1), :].rearrange("(p j) c -> p j c", j=PACK)
+                nc.sync.dma_start(out=raws[w, b][:, a, :, :], in_=rows[:, :, P * b : P * (b + 1)])
+
+        def load_weights(b):
+            load_weight(0, b)
+            load_weight(1, b)
 
         w2_w = kept([P, PASSES, 2 * H], U8, "w2_w")
-        wgs_t = kept([P, S], F32, "wgs_t")
+        wgs_t = [kept([P, HALF], F32, "wgs_t%d" % h) for h in range(HALVES)]
         pages = [kept([P, T2], F32, "page%d" % b) for b in range(BLOCKS)]
         gain_t = kept([P, BLOCKS], F32, "gain_t")
         w4_raw = kept([P, N], I32, "w4_raw")
@@ -97,28 +98,32 @@ def tile_list_carousel_greasing_log_kernel(
         def load_page(b):
             nc.sync.dma_start(out=pages[b][:], in_=page0[P * b : P * (b + 1), :])
 
-        load_weights(spans[0])
         load_tab(1)
+        load_weight(0, 0)
+        nc.sync.dma_start(out=w2_w[:].bitcast(I32), in_=w2_words.rearrange("a p c -> p a c").bitcast(I32))
+        load_weight(1, 0)
 
-        got_w = [[kept([P, HALF], U32, "got_w%d_%d" % (a, h)) for h in range(HALVES)] for a in range(PASSES)]
+        got_w = {}
         got_s = kept([P, S], U8, "got_s")
 
         def half_of(idx, h):
             return idx[:, LIST_COLS * h : LIST_COLS * (h + 1)]
 
-        def gather_words(a, h):
-            nc.vector.tensor_copy(got_w[a][h][:], tab_w[a][:].bitcast(U32).indirect(half_of(idx1, h)))
+        def gather_words(a, h, tag=""):
+            got_w[a, h] = kept([P, HALF], U32, "got_w%d_%d" % (a, h), tag=tag)
+            nc.vector.tensor_copy(got_w[a, h][:], tab_w[a][:].bitcast(U32).indirect(half_of(idx1, h)))
 
         w_codes = {}
         w_scales = {}
 
         def quantise_weight(w, b):
             raw = raws[w, b]
-            rounded = kept([P, PASSES, P, PACK], BF16, "w_rounded%d_%d" % (w, b), tag="w_rounded%d_%d" % (w, b % 2))
-            nc.scalar.copy(
-                out=rounded[:].rearrange("p a (c i) j -> p a c j i", i=4),
-                in_=raw.rearrange("p a j (c i) -> p a c j i", i=4),
-            )
+            rounded = kept([P, PASSES, P, PACK], BF16, "w_rounded%d_%d" % (w, b), tag=("first%d", "prod%d")[w] % (b - 1))
+            for part in ((slice(0, 1), slice(1, 2)) if b == 0 else (slice(0, PASSES),)):
+                nc.scalar.copy(
+                    out=rounded[:, part].rearrange("p a (c i) j -> p a c j i", i=4),
+                    in_=raw[:, part].rearrange("p a j (c i) -> p a c j i", i=4),
+                )
             w_codes[w, b] = kept([P, PASSES, P], U32, "w_codes%d_%d" % (w, b))
             w_scales[w, b] = kept([P, PASSES, P], U8, "w_scales%d_%d" % (w, b))
             nc.vector.quantize_mx(
@@ -134,22 +139,23 @@ def tile_list_carousel_greasing_log_kernel(
                 out=got_s1[32 * q : 32 * q + 4, :].bitcast(I32),
                 in_=got_s[32 * q + 4 : 32 * q + 8, :].bitcast(I32),
             )
+        gather_words(1, 0)
         quantise_weight(0, 0)
         quantise_weight(1, 0)
-        gather_words(1, 0)
-        gather_words(0, 1)
-        gather_words(1, 1)
+        gather_words(1, 1, tag="first-1")
+        gather_words(0, 1, tag="prod-1")
 
-        nc.sync.dma_start(out=w2_w[:].bitcast(I32), in_=w2_words.rearrange("a p c -> p a c").bitcast(I32))
         nc.sync.dma_start(idx2[:], offs2)
-        nc.sync.dma_start(out=wgs_t[:], in_=wgs)
-        load_page(0)
-        load_weights(spans[1])
-        load_weights(spans[2])
-        load_page(1)
         nc.sync.dma_start(idx3[:], offs3)
+        nc.sync.dma_start(out=wgs_t[0][:], in_=wgs[:, 0:HALF])
         with nc.allow_non_contiguous_dma(reason="one gain for each row of a block, rows on the partitions"):
             nc.sync.dma_start(out=gain_t[:], in_=gain.rearrange("(b p) -> p b", p=P))
+        load_page(0)
+        load_weights(1)
+        nc.sync.dma_start(out=wgs_t[1][:], in_=wgs[:, HALF:S])
+        load_weights(2)
+        load_page(1)
+        load_weights(3)
         load_page(2)
         load_page(3)
         nc.sync.dma_start(out=w5_raw[:], in_=w5.rearrange("(p j) c -> p j c", j=PACK))
@@ -162,38 +168,48 @@ def tile_list_carousel_greasing_log_kernel(
 
         def products(b, h):
             cols = slice(HALF * h, HALF * (h + 1))
-            first = psum.tile([P, HALF], F32, name="bank_a")
-            second = psum.tile([P, HALF], F32, name="bank_b")
-            third = psum.tile([P, HALF], F32, name="bank_c")
-            for w, bank in ((0, first), (1, third)):
+            first, second, third = [
+                psum.tile([P, HALF], F32, name="sum%d_%d_%d" % (b, h, i), tag="bank%d" % (3 * h + i))[:] for i in range(3)
+            ]
+
+            def quantised_weight(w, bank):
                 for a in range(PASSES):
                     nc.tensor.matmul_mx(
-                        out=bank[:],
+                        out=bank,
                         lhsT=w_codes[w, b][:, a, :].bitcast(FP8X4),
                         lhsT_scale=w_scales[w, b][:, a, :],
-                        rhs=got_w[a][h][:].bitcast(FP8X4),
+                        rhs=got_w[a, h][:].bitcast(FP8X4),
                         rhs_scale=got_s[4 * a : P, cols],
                         start=(a == 0),
                         stop=(a == PASSES - 1),
                     )
+
+            quantised_weight(0, first)
             for a in range(PASSES):
                 nc.tensor.matmul_mx(
-                    out=second[:],
+                    out=second,
                     lhsT=w2_w[:, a, 2 * P * b : 2 * P * (b + 1)].bitcast(FP4X4),
                     lhsT_scale=w2_s[:, a, P * b : P * (b + 1)],
-                    rhs=got_w[a][h][:].bitcast(FP8X4),
+                    rhs=got_w[a, h][:].bitcast(FP8X4),
                     rhs_scale=(got_s, got_s1)[a][:, cols],
                     start=(a == 0),
                     stop=(a == PASSES - 1),
                 )
-            first_sb = ring.tile([P, HALF], F32, name="first_sb")
-            nc.scalar.copy(out=first_sb[:], in_=first[:])
-            prod = kept([P, HALF], F32, "prod%d_%d" % (b, h), tag="prod%d_%d" % (b % 2, h))
-            nc.vector.tensor_tensor(prod[:], second[:], first_sb[:], ALU.mult)
-            return prod, third
+            quantised_weight(1, third)
+            first_sb = kept([P, HALF], F32, "first_sb%d_%d" % (b, h), tag="first%d" % (2 * b + h))
+            nc.scalar.copy(out=first_sb[:], in_=first)
+            after = b if (h == 1 and 0 < b < BLOCKS - 1) else 2 * b + h
+            prod = kept([P, HALF], F32, "prod%d_%d" % (b, h), tag="prod%d" % after)
+            nc.vector.tensor_tensor(prod[:], second, first_sb[:], ALU.mult)
+            return prod, third, first_sb
 
-        def add_third(h_cols, prod, third):
-            nc.vector.tensor_tensor(h_cols, third[:], prod[:], ALU.add)
+        def add_third(h_cols, prod, third, first_sb):
+            nc.vector.tensor_tensor(h_cols, third, prod[:], ALU.add)
+
+        def add_third_aside(h_cols, prod, third, first_sb):
+            third_sb = ring.tile([P, HALF], F32, name="third_sb")
+            nc.scalar.copy(out=third_sb[:], in_=third)
+            nc.gpsimd.tensor_tensor(h_cols, third_sb[:], prod[:], ALU.add)
 
         z_rows = [kept([P, PACK, HALF], BF16, "z_rows%d" % h) for h in range(HALVES)]
 
@@ -216,35 +232,38 @@ def tile_list_carousel_greasing_log_kernel(
         h_first = kept([P, HALF], F32, "h_first")
         add_third(h_first[:], *parts)
         parts = products(0, 1)
-        nc.vector.tensor_tensor(pages[0][:].indirect(half_of(idx2, 0)), h_first[:], wgs_t[:, 0:HALF], ALU.mult)
+        nc.vector.tensor_tensor(pages[0][:].indirect(half_of(idx2, 0)), h_first[:], wgs_t[0][:], ALU.mult)
         quantise_weight(0, 1)
         quantise_weight(1, 1)
-        h_second = kept([P, HALF], F32, "h_second", tag="w_rounded1_1")
+        h_second = kept([P, HALF], F32, "h_second", tag="prod0")
         add_third(h_second[:], *parts)
-        nc.vector.tensor_tensor(pages[0][:].indirect(half_of(idx2, 1)), h_second[:], wgs_t[:, HALF:S], ALU.mult)
+        nc.vector.tensor_tensor(pages[0][:].indirect(half_of(idx2, 1)), h_second[:], wgs_t[1][:], ALU.mult)
         for b in range(1, BLOCKS):
             if b + 1 < BLOCKS:
                 quantise_weight(0, b + 1)
                 quantise_weight(1, b + 1)
             both = [products(b, h) for h in range(HALVES)]
-            h_sb = kept([P, S], F32, "h_sb%d" % b, tag="h_sb")
+            h_sb = [kept([P, HALF], F32, "h_sb%d_%d" % (b, h), tag="h_sb%d" % h) for h in range(HALVES)]
             for h in range(HALVES):
-                add_third(h_sb[:, HALF * h : HALF * (h + 1)], *both[h])
-            look(b - 1, both[1][0][:, 0:1])
-            nc.vector.tensor_tensor(pages[b][:].indirect(idx2[:]), h_sb[:], wgs_t[:], ALU.mult)
+                add_third_aside(h_sb[h][:], *both[h])
+            look(b - 1, both[1][2][:, 0:1])
+            for h in range(HALVES):
+                nc.vector.tensor_tensor(
+                    pages[b][:].indirect(half_of(idx2, h)), h_sb[h][:], wgs_t[h][:], ALU.mult
+                )
         last_top = kept([P, 1], F32, "last_top")
         look(BLOCKS - 1, last_top[:])
 
-        w4_w = kept([P, PACK, P], I32, "w4_w")
-        w4_s = kept([P, PACK, P], U8, "w4_s", tag="wgs_t")
+        w4_w = kept([P, PACK, P], I32, "w4_w", tag="first4")
+        w4_s = kept([P, PACK, P], U8, "w4_s", tag="wgs_t1")
         nc.scalar.copy(out=w4_w[:].bitcast(U32), in_=w4_raw[:].bitcast(U32).rearrange("p (m t) -> p t m", t=PACK))
         nc.vector.tensor_copy(out=w4_s[:], in_=w4_s_raw[:].rearrange("p (m t) -> p t m", t=PACK))
-        w5_rounded = kept([P, PACK, P, PACK], BF16, "w5_rounded")
+        w5_rounded = kept([P, PACK, P, PACK], BF16, "w5_rounded", tag="prod4")
         nc.scalar.copy(
             out=w5_rounded[:].rearrange("p t m j -> p m t j"),
             in_=w5_raw[:].rearrange("p j (m t) -> p m t j", t=PACK),
         )
-        w5_w = kept([P, PACK, P], U32, "w5_w", tag="h_sb")
+        w5_w = kept([P, PACK, P], U32, "w5_w", tag="h_sb1")
         w5_s = kept([P, PACK, P], U8, "w5_s")
         nc.vector.quantize_mx(
             out=w5_w[:].rearrange("p t m -> p (t m)").bitcast(FP8X4),
@@ -259,8 +278,9 @@ def tile_list_carousel_greasing_log_kernel(
 
         def quantise_z(c):
             h, lo = divmod(CHUNK * c, HALF)
-            z_in = ring.tile([P, CHUNK, PACK], BF16, name="z_in", align_bytes=64)
-            nc.vector.tensor_copy(
+            z_in = kept([P, CHUNK, PACK], BF16, "z_in%d" % c)
+            weave = nc.scalar.copy if c in S_WEAVES else nc.vector.tensor_copy
+            weave(
                 out=z_in[:].rearrange("p (c i) t -> p c t i", i=4),
                 in_=z_rows[h][:, :, lo : lo + CHUNK].rearrange("p t (c i) -> p c t i", i=4),
             )
@@ -272,8 +292,11 @@ def tile_list_carousel_greasing_log_kernel(
         def second_stage(c, z_w, z_s):
             y = kept([P, PACK, CHUNK], F32, "y%d" % c)
             for pair in range(2):
-                plain = psum.tile([P, 2, CHUNK], F32, name=("bank_a", "bank_b")[pair])
-                other = psum.tile([P, 2, CHUNK], F32, name=("bank_c", "bank_d")[pair])
+                at = 4 * (c % 2) + 2 * pair
+                plain = psum.tile([P, 2, CHUNK], F32, name="plain%d_%d" % (c, pair), tag="bank%d" % at)
+                other = psum.tile(
+                    [P, 2, CHUNK], F32, name="other%d_%d" % (c, pair), tag="bank%d" % (at + 1)
+                )
                 for codes, scales, bank in ((w5_w, w5_s, other), (w4_w, w4_s, plain)):
                     for i in range(2):
                         t = 2 * pair + i
@@ -296,7 +319,7 @@ def tile_list_carousel_greasing_log_kernel(
         def planes(c, y):
             cols = slice(CHUNK * c, CHUNK * (c + 1))
             y_in = ring.tile([P, CHUNK, PACK], BF16, name="y_in", align_bytes=64)
-            cast = nc.vector.tensor_copy if c == M // CHUNK - 1 else nc.scalar.copy
+            cast = nc.scalar.copy if c in S_CASTS else nc.vector.tensor_copy
             cast(
                 out=y_in[:].rearrange("p (c i) t -> p c t i", i=4),
                 in_=y[:].rearrange("p t (c i) -> p c t i", i=4),
@@ -307,10 +330,12 @@ def tile_list_carousel_greasing_log_kernel(
             nc.sync.dma_start(out=out_words[:, cols], in_=y_words[:, cols])
 
         chunks = M // CHUNK
-        zq = [quantise_z(c) for c in range(chunks)]
+        zq = [quantise_z(0), quantise_z(1)]
         ys = []
         for c in range(chunks):
             ys.append(second_stage(c, *zq[c]))
+            if c + 2 < chunks:
+                zq.append(quantise_z(c + 2))
             if c > 0:
                 planes(c - 1, ys[c - 1])
         planes(chunks - 1, ys[chunks - 1])

@@ -19,15 +19,20 @@ FLOPS = 2 * K * H * S * 3 + 2 * H * N * M * 2
 
 P = 128
 PACK = 4
-PASSES = K // (P * PACK)
+K_PASS = P * PACK
+PASSES = K // K_PASS
 BLOCKS = H // P
 HALF = 512
 HALVES = S // HALF
 LIST_COLS = HALF // 16
-CHUNK = 256
 QUADS = 4
-S_WEAVES = ()
-S_CASTS = (0, 1, 2)
+QUAD = P // QUADS
+SCALE_ROWS = 4
+LINE = 4
+CHUNK = 256
+CHUNKS = M // CHUNK
+SCALAR_Z_CHUNKS = (1,)
+SCALAR_Y_CHUNKS = (0, 1)
 
 
 def tile_list_carousel_greasing_log_kernel(
@@ -62,17 +67,23 @@ def tile_list_carousel_greasing_log_kernel(
         def load_tab(a):
             nc.sync.dma_start(out=tab_w[a][:], in_=tab_words[a].rearrange("p t i -> p (t i)").bitcast(I32))
 
+        def scale_rows(q):
+            return slice(SCALE_ROWS * q, SCALE_ROWS * (q + 1))
+
+        def scale_partitions(q):
+            return slice(QUAD * q, QUAD * q + SCALE_ROWS)
+
         nc.sync.dma_start(idx1[:], offs)
         load_tab(0)
         for q in range(QUADS):
             nc.sync.dma_start(
-                out=tab_s[32 * q : 32 * q + 4 * PASSES, :].bitcast(I32),
-                in_=tab_scales[:, 4 * q : 4 * q + 4, :].bitcast(I32),
+                out=tab_s[QUAD * q : QUAD * q + SCALE_ROWS * PASSES, :].bitcast(I32),
+                in_=tab_scales[:, scale_rows(q), :].bitcast(I32),
             )
         for q in range(QUADS):
             nc.gpsimd.dma_start(
-                out=w2_s[32 * q : 32 * q + 4, :, :].bitcast(I32),
-                in_=w2_scales[:, 4 * q : 4 * q + 4, :].rearrange("a r c -> r a c").bitcast(I32),
+                out=w2_s[scale_partitions(q), :, :].bitcast(I32),
+                in_=w2_scales[:, scale_rows(q), :].rearrange("a r c -> r a c").bitcast(I32),
             )
 
         weights = (w1, w3)
@@ -81,7 +92,7 @@ def tile_list_carousel_greasing_log_kernel(
         def load_weight(w, b):
             raws[w, b] = kept([P, PASSES, PACK, P], F32, "raw%d_%d" % (w, b))
             for a in range(PASSES):
-                rows = weights[w][512 * a : 512 * (a + 1), :].rearrange("(p j) c -> p j c", j=PACK)
+                rows = weights[w][K_PASS * a : K_PASS * (a + 1), :].rearrange("(p j) c -> p j c", j=PACK)
                 nc.sync.dma_start(out=raws[w, b][:, a, :, :], in_=rows[:, :, P * b : P * (b + 1)])
 
         def load_weights(b):
@@ -116,13 +127,20 @@ def tile_list_carousel_greasing_log_kernel(
         w_codes = {}
         w_scales = {}
 
+        def first_tag(unit):
+            return "first%d" % unit
+
+        def prod_tag(unit):
+            return "prod%d" % unit
+
         def quantise_weight(w, b):
-            raw = raws[w, b]
-            rounded = kept([P, PASSES, P, PACK], BF16, "w_rounded%d_%d" % (w, b), tag=("first%d", "prod%d")[w] % (b - 1))
-            for part in ((slice(0, 1), slice(1, 2)) if b == 0 else (slice(0, PASSES),)):
+            tag = (first_tag, prod_tag)[w](b - 1)
+            rounded = kept([P, PASSES, P, PACK], BF16, "w_rounded%d_%d" % (w, b), tag=tag)
+            parts = [slice(a, a + 1) for a in range(PASSES)] if b == 0 else [slice(0, PASSES)]
+            for part in parts:
                 nc.scalar.copy(
-                    out=rounded[:, part].rearrange("p a (c i) j -> p a c j i", i=4),
-                    in_=raw[:, part].rearrange("p a j (c i) -> p a c j i", i=4),
+                    out=rounded[:, part].rearrange("p a (c i) j -> p a c j i", i=LINE),
+                    in_=raws[w, b][:, part].rearrange("p a j (c i) -> p a c j i", i=LINE),
                 )
             w_codes[w, b] = kept([P, PASSES, P], U32, "w_codes%d_%d" % (w, b))
             w_scales[w, b] = kept([P, PASSES, P], U8, "w_scales%d_%d" % (w, b))
@@ -136,23 +154,23 @@ def tile_list_carousel_greasing_log_kernel(
         nc.vector.tensor_copy(got_s[:], tab_s[:].indirect(idx1[:]))
         for q in range(QUADS):
             nc.sync.dma_start(
-                out=got_s1[32 * q : 32 * q + 4, :].bitcast(I32),
-                in_=got_s[32 * q + 4 : 32 * q + 8, :].bitcast(I32),
+                out=got_s1[scale_partitions(q), :].bitcast(I32),
+                in_=got_s[QUAD * q + SCALE_ROWS : QUAD * q + 2 * SCALE_ROWS, :].bitcast(I32),
             )
         gather_words(1, 0)
         quantise_weight(0, 0)
         quantise_weight(1, 0)
-        gather_words(1, 1, tag="first-1")
-        gather_words(0, 1, tag="prod-1")
+        gather_words(1, 1, tag=first_tag(-1))
+        gather_words(0, 1, tag=prod_tag(-1))
 
         nc.sync.dma_start(idx2[:], offs2)
         nc.sync.dma_start(idx3[:], offs3)
         nc.sync.dma_start(out=wgs_t[0][:], in_=wgs[:, 0:HALF])
-        with nc.allow_non_contiguous_dma(reason="one gain for each row of a block, rows on the partitions"):
-            nc.sync.dma_start(out=gain_t[:], in_=gain.rearrange("(b p) -> p b", p=P))
         load_page(0)
         load_weights(1)
         nc.sync.dma_start(out=wgs_t[1][:], in_=wgs[:, HALF:S])
+        with nc.allow_non_contiguous_dma(reason="one gain for each row of a block, rows on the partitions"):
+            nc.sync.dma_start(out=gain_t[:], in_=gain.rearrange("(b p) -> p b", p=P))
         load_weights(2)
         load_page(1)
         load_weights(3)
@@ -162,29 +180,30 @@ def tile_list_carousel_greasing_log_kernel(
         nc.sync.dma_start(out=w4_raw[:], in_=w4_words[0].rearrange("p c i -> p (c i)").bitcast(I32))
         for q in range(QUADS):
             nc.sync.dma_start(
-                out=w4_s_raw[32 * q : 32 * q + 4, :].bitcast(I32),
-                in_=w4_scales[0, 4 * q : 4 * q + 4, :].bitcast(I32),
+                out=w4_s_raw[scale_partitions(q), :].bitcast(I32),
+                in_=w4_scales[0, scale_rows(q), :].bitcast(I32),
             )
 
         def products(b, h):
             cols = slice(HALF * h, HALF * (h + 1))
             first, second, third = [
-                psum.tile([P, HALF], F32, name="sum%d_%d_%d" % (b, h, i), tag="bank%d" % (3 * h + i))[:] for i in range(3)
+                psum.tile([P, HALF], F32, name="sum%d_%d_%d" % (b, h, i), tag="bank%d" % (3 * h + i))[:]
+                for i in range(3)
             ]
 
-            def quantised_weight(w, bank):
+            def multiply_by_weight(w, bank):
                 for a in range(PASSES):
                     nc.tensor.matmul_mx(
                         out=bank,
                         lhsT=w_codes[w, b][:, a, :].bitcast(FP8X4),
                         lhsT_scale=w_scales[w, b][:, a, :],
                         rhs=got_w[a, h][:].bitcast(FP8X4),
-                        rhs_scale=got_s[4 * a : P, cols],
+                        rhs_scale=got_s[SCALE_ROWS * a : P, cols],
                         start=(a == 0),
                         stop=(a == PASSES - 1),
                     )
 
-            quantised_weight(0, first)
+            multiply_by_weight(0, first)
             for a in range(PASSES):
                 nc.tensor.matmul_mx(
                     out=second,
@@ -195,21 +214,16 @@ def tile_list_carousel_greasing_log_kernel(
                     start=(a == 0),
                     stop=(a == PASSES - 1),
                 )
-            quantised_weight(1, third)
-            first_sb = kept([P, HALF], F32, "first_sb%d_%d" % (b, h), tag="first%d" % (2 * b + h))
+            multiply_by_weight(1, third)
+            first_sb = kept([P, HALF], F32, "first_sb%d_%d" % (b, h), tag=first_tag(2 * b + h))
             nc.scalar.copy(out=first_sb[:], in_=first)
-            after = b if (h == 1 and 0 < b < BLOCKS - 1) else 2 * b + h
-            prod = kept([P, HALF], F32, "prod%d_%d" % (b, h), tag="prod%d" % after)
+            follows_next_weights = h == HALVES - 1 and 0 < b < BLOCKS - 1
+            prod = kept([P, HALF], F32, "prod%d_%d" % (b, h), tag=prod_tag(b if follows_next_weights else 2 * b + h))
             nc.vector.tensor_tensor(prod[:], second, first_sb[:], ALU.mult)
             return prod, third, first_sb
 
-        def add_third(h_cols, prod, third, first_sb):
-            nc.vector.tensor_tensor(h_cols, third, prod[:], ALU.add)
-
-        def add_third_aside(h_cols, prod, third, first_sb):
-            third_sb = ring.tile([P, HALF], F32, name="third_sb")
-            nc.scalar.copy(out=third_sb[:], in_=third)
-            nc.gpsimd.tensor_tensor(h_cols, third_sb[:], prod[:], ALU.add)
+        def put(b, h, h_sb):
+            nc.vector.tensor_tensor(pages[b][:].indirect(half_of(idx2, h)), h_sb[:], wgs_t[h][:], ALU.mult)
 
         z_rows = [kept([P, PACK, HALF], BF16, "z_rows%d" % h) for h in range(HALVES)]
 
@@ -226,18 +240,19 @@ def tile_list_carousel_greasing_log_kernel(
                 else:
                     nc.scalar.activation(out=z_sb[:], in_=a_sb[:], func=ACT.Copy, scale=gain_t[:, b : b + 1])
                 for t in range(PACK):
-                    nc.sync.dma_start(out=z_rows[h][32 * b : 32 * (b + 1), t, :], in_=z_sb[t:P:PACK, :])
+                    nc.sync.dma_start(out=z_rows[h][QUAD * b : QUAD * (b + 1), t, :], in_=z_sb[t:P:PACK, :])
 
-        parts = products(0, 0)
+        prod, third = products(0, 0)[:2]
         h_first = kept([P, HALF], F32, "h_first")
-        add_third(h_first[:], *parts)
-        parts = products(0, 1)
-        nc.vector.tensor_tensor(pages[0][:].indirect(half_of(idx2, 0)), h_first[:], wgs_t[0][:], ALU.mult)
+        nc.vector.tensor_tensor(h_first[:], third, prod[:], ALU.add)
+        prod, third = products(0, 1)[:2]
+        put(0, 0, h_first)
         quantise_weight(0, 1)
         quantise_weight(1, 1)
-        h_second = kept([P, HALF], F32, "h_second", tag="prod0")
-        add_third(h_second[:], *parts)
-        nc.vector.tensor_tensor(pages[0][:].indirect(half_of(idx2, 1)), h_second[:], wgs_t[1][:], ALU.mult)
+        h_second = kept([P, HALF], F32, "h_second", tag=prod_tag(0))
+        nc.vector.tensor_tensor(h_second[:], third, prod[:], ALU.add)
+        put(0, 1, h_second)
+
         for b in range(1, BLOCKS):
             if b + 1 < BLOCKS:
                 quantise_weight(0, b + 1)
@@ -245,24 +260,22 @@ def tile_list_carousel_greasing_log_kernel(
             both = [products(b, h) for h in range(HALVES)]
             h_sb = [kept([P, HALF], F32, "h_sb%d_%d" % (b, h), tag="h_sb%d" % h) for h in range(HALVES)]
             for h in range(HALVES):
-                add_third_aside(h_sb[h][:], *both[h])
-            look(b - 1, both[1][2][:, 0:1])
+                prod, third = both[h][:2]
+                third_sb = ring.tile([P, HALF], F32, name="third_sb")
+                nc.scalar.copy(out=third_sb[:], in_=third)
+                nc.gpsimd.tensor_tensor(h_sb[h][:], third_sb[:], prod[:], ALU.add)
+            look(b - 1, both[HALVES - 1][2][:, 0:1])
             for h in range(HALVES):
-                nc.vector.tensor_tensor(
-                    pages[b][:].indirect(half_of(idx2, h)), h_sb[h][:], wgs_t[h][:], ALU.mult
-                )
+                put(b, h, h_sb[h])
         last_top = kept([P, 1], F32, "last_top")
         look(BLOCKS - 1, last_top[:])
 
-        w4_w = kept([P, PACK, P], I32, "w4_w", tag="first4")
+        w4_w = kept([P, PACK, P], I32, "w4_w", tag=first_tag(2 * (BLOCKS - 2)))
         w4_s = kept([P, PACK, P], U8, "w4_s", tag="wgs_t1")
         nc.scalar.copy(out=w4_w[:].bitcast(U32), in_=w4_raw[:].bitcast(U32).rearrange("p (m t) -> p t m", t=PACK))
         nc.vector.tensor_copy(out=w4_s[:], in_=w4_s_raw[:].rearrange("p (m t) -> p t m", t=PACK))
-        w5_rounded = kept([P, PACK, P, PACK], BF16, "w5_rounded", tag="prod4")
-        nc.scalar.copy(
-            out=w5_rounded[:].rearrange("p t m j -> p m t j"),
-            in_=w5_raw[:].rearrange("p j (m t) -> p m t j", t=PACK),
-        )
+        w5_rounded = kept([P, PACK, P, PACK], BF16, "w5_rounded", tag=prod_tag(2 * (BLOCKS - 1)))
+        nc.scalar.copy(out=w5_rounded[:], in_=w5_raw[:].rearrange("p j (m t) -> p t m j", t=PACK))
         w5_w = kept([P, PACK, P], U32, "w5_w", tag="h_sb1")
         w5_s = kept([P, PACK, P], U8, "w5_s")
         nc.vector.quantize_mx(
@@ -276,14 +289,17 @@ def tile_list_carousel_greasing_log_kernel(
         out_rows = out_0.rearrange("(p t) m -> p t m", t=PACK)
         out_words = out_1[0].rearrange("p m t -> p (m t)").bitcast(I32)
 
+        def interleave(on_scalar, out, rows):
+            copy = nc.scalar.copy if on_scalar else nc.vector.tensor_copy
+            copy(
+                out=out.rearrange("p (c i) t -> p c t i", i=LINE),
+                in_=rows.rearrange("p t (c i) -> p c t i", i=LINE),
+            )
+
         def quantise_z(c):
             h, lo = divmod(CHUNK * c, HALF)
             z_in = kept([P, CHUNK, PACK], BF16, "z_in%d" % c)
-            weave = nc.scalar.copy if c in S_WEAVES else nc.vector.tensor_copy
-            weave(
-                out=z_in[:].rearrange("p (c i) t -> p c t i", i=4),
-                in_=z_rows[h][:, :, lo : lo + CHUNK].rearrange("p t (c i) -> p c t i", i=4),
-            )
+            interleave(c in SCALAR_Z_CHUNKS, z_in[:], z_rows[h][:, :, lo : lo + CHUNK])
             z_w = kept([P, CHUNK], U32, "z_w%d" % c)
             z_s = kept([P, CHUNK], U8, "z_s%d" % c)
             nc.vector.quantize_mx(out=z_w[:].bitcast(FP8X4), scales=z_s[:], in_=z_in[:].rearrange("p m t -> p (m t)"))
@@ -291,12 +307,10 @@ def tile_list_carousel_greasing_log_kernel(
 
         def second_stage(c, z_w, z_s):
             y = kept([P, PACK, CHUNK], F32, "y%d" % c)
-            for pair in range(2):
+            for pair in range(PACK // 2):
                 at = 4 * (c % 2) + 2 * pair
                 plain = psum.tile([P, 2, CHUNK], F32, name="plain%d_%d" % (c, pair), tag="bank%d" % at)
-                other = psum.tile(
-                    [P, 2, CHUNK], F32, name="other%d_%d" % (c, pair), tag="bank%d" % (at + 1)
-                )
+                other = psum.tile([P, 2, CHUNK], F32, name="other%d_%d" % (c, pair), tag="bank%d" % (at + 1))
                 for codes, scales, bank in ((w5_w, w5_s, other), (w4_w, w4_s, plain)):
                     for i in range(2):
                         t = 2 * pair + i
@@ -319,27 +333,22 @@ def tile_list_carousel_greasing_log_kernel(
         def planes(c, y):
             cols = slice(CHUNK * c, CHUNK * (c + 1))
             y_in = ring.tile([P, CHUNK, PACK], BF16, name="y_in", align_bytes=64)
-            cast = nc.scalar.copy if c in S_CASTS else nc.vector.tensor_copy
-            cast(
-                out=y_in[:].rearrange("p (c i) t -> p c t i", i=4),
-                in_=y[:].rearrange("p t (c i) -> p c t i", i=4),
-            )
+            interleave(c in SCALAR_Y_CHUNKS, y_in[:], y[:])
             nc.vector.quantize_mx(
                 out=y_words[:, cols].bitcast(FP8X4), scales=y_scales[:, cols], in_=y_in[:].rearrange("p m t -> p (m t)")
             )
             nc.sync.dma_start(out=out_words[:, cols], in_=y_words[:, cols])
 
-        chunks = M // CHUNK
         zq = [quantise_z(0), quantise_z(1)]
         ys = []
-        for c in range(chunks):
+        for c in range(CHUNKS):
             ys.append(second_stage(c, *zq[c]))
-            if c + 2 < chunks:
+            if c + 2 < CHUNKS:
                 zq.append(quantise_z(c + 2))
             if c > 0:
                 planes(c - 1, ys[c - 1])
-        planes(chunks - 1, ys[chunks - 1])
+        planes(CHUNKS - 1, ys[CHUNKS - 1])
         for q in range(QUADS):
             nc.scalar.dma_start(
-                out=out_2[0, 4 * q : 4 * q + 4, :].bitcast(I32), in_=y_scales[32 * q : 32 * q + 4, :].bitcast(I32)
+                out=out_2[0, scale_rows(q), :].bitcast(I32), in_=y_scales[scale_partitions(q), :].bitcast(I32)
             )

from contextlib import ExitStack

import concourse.mybir as mybir

F32 = mybir.dt.float32
BF16 = mybir.dt.bfloat16
I32 = mybir.dt.int32
U32 = mybir.dt.uint32
U16 = mybir.dt.uint16
U8 = mybir.dt.uint8
FP8X4 = mybir.dt.float8_e4m3fn_x4
FP4X4 = mybir.dt.float4_e2m1fn_x4
ALU = mybir.AluOpType
ACT = mybir.ActivationFunctionType
AXIS = mybir.AxisListType

K, H, N, T, S, T2, M = 1024, 512, 512, 2048, 1024, 2048, 1024
FLOPS = 2 * K * H * S * 3 + 2 * H * N * M * 2

P = 128
PACK = 4
K_PASS = P * PACK
PASSES = K // K_PASS
BLOCKS = H // P
HALF = 512
HALVES = S // HALF
LIST_COLS = HALF // 16
QUADS = 4
QUAD = P // QUADS
SCALE_ROWS = 4
LINE = 4
CHUNK = 256
CHUNKS = M // CHUNK
SCALAR_Z_CHUNKS = (1,)
SCALAR_Y_CHUNKS = (0, 1)


def tile_list_carousel_greasing_log_kernel(
    tc, tab_words, tab_scales, offs, offs2, offs3, w1, w2_words, w2_scales, w3, page0, wgs, gain,
    w4_words, w4_scales, w5, out_0, out_1, out_2,
):
    nc = tc.nc
    with ExitStack() as ctx:
        lists = ctx.enter_context(tc.tile_pool(name="lists", bufs=1))
        keep = ctx.enter_context(tc.tile_pool(name="keep", bufs=1))
        ring = ctx.enter_context(tc.tile_pool(name="ring", bufs=2))
        psum = ctx.enter_context(tc.psum_pool(name="psum", bufs=1))

        def kept(shape, dtype, name, tag=""):
            return keep.tile(shape, dtype, name=name, tag=tag or name, align_bytes=64)

        idx1 = lists.tile([P, S // 16], U16, name="idx1")
        idx2 = lists.tile([P, S // 16], U16, name="idx2")
        idx3 = lists.tile([P, M // 16], U16, name="idx3")

        tab_s = kept([P, T], U8, "tab_s")
        got_s1 = kept([P, S], U8, "got_s1")
        w2_s = kept([P, PASSES, H], U8, "w2_s")
        w4_s_raw = kept([P, N], U8, "w4_s_raw")
        nc.vector.memset(tab_s[:].bitcast(I32), 0)
        nc.vector.memset(w2_s[:].rearrange("p a c -> p (a c)").bitcast(I32), 0)
        nc.vector.memset(got_s1[:].bitcast(I32), 0)
        nc.vector.memset(w4_s_raw[:].bitcast(I32), 0)

        tab_w = [kept([P, T], I32, "tab_w%d" % a) for a in range(PASSES)]

        def load_tab(a):
            nc.sync.dma_start(out=tab_w[a][:], in_=tab_words[a].rearrange("p t i -> p (t i)").bitcast(I32))

        def scale_rows(q):
            return slice(SCALE_ROWS * q, SCALE_ROWS * (q + 1))

        def scale_partitions(q):
            return slice(QUAD * q, QUAD * q + SCALE_ROWS)

        nc.sync.dma_start(idx1[:], offs)
        load_tab(0)
        for q in range(QUADS):
            nc.sync.dma_start(
                out=tab_s[QUAD * q : QUAD * q + SCALE_ROWS * PASSES, :].bitcast(I32),
                in_=tab_scales[:, scale_rows(q), :].bitcast(I32),
            )
        for q in range(QUADS):
            nc.gpsimd.dma_start(
                out=w2_s[scale_partitions(q), :, :].bitcast(I32),
                in_=w2_scales[:, scale_rows(q), :].rearrange("a r c -> r a c").bitcast(I32),
            )

        weights = (w1, w3)
        raws = {}

        def load_weight(w, b):
            raws[w, b] = kept([P, PASSES, PACK, P], F32, "raw%d_%d" % (w, b))
            for a in range(PASSES):
                rows = weights[w][K_PASS * a : K_PASS * (a + 1), :].rearrange("(p j) c -> p j c", j=PACK)
                nc.sync.dma_start(out=raws[w, b][:, a, :, :], in_=rows[:, :, P * b : P * (b + 1)])

        def load_weights(b):
            load_weight(0, b)
            load_weight(1, b)

        w2_w = kept([P, PASSES, 2 * H], U8, "w2_w")
        wgs_t = [kept([P, HALF], F32, "wgs_t%d" % h) for h in range(HALVES)]
        pages = [kept([P, T2], F32, "page%d" % b) for b in range(BLOCKS)]
        gain_t = kept([P, BLOCKS], F32, "gain_t")
        w4_raw = kept([P, N], I32, "w4_raw")
        w5_raw = kept([P, PACK, N], F32, "w5_raw")

        def load_page(b):
            nc.sync.dma_start(out=pages[b][:], in_=page0[P * b : P * (b + 1), :])

        load_tab(1)
        load_weight(0, 0)
        nc.sync.dma_start(out=w2_w[:].bitcast(I32), in_=w2_words.rearrange("a p c -> p a c").bitcast(I32))
        load_weight(1, 0)

        got_w = {}
        got_s = kept([P, S], U8, "got_s")

        def half_of(idx, h):
            return idx[:, LIST_COLS * h : LIST_COLS * (h + 1)]

        def gather_words(a, h, tag=""):
            got_w[a, h] = kept([P, HALF], U32, "got_w%d_%d" % (a, h), tag=tag)
            nc.vector.tensor_copy(got_w[a, h][:], tab_w[a][:].bitcast(U32).indirect(half_of(idx1, h)))

        w_codes = {}
        w_scales = {}

        def first_tag(unit):
            return "first%d" % unit

        def prod_tag(unit):
            return "prod%d" % unit

        def quantise_weight(w, b):
            tag = (first_tag, prod_tag)[w](b - 1)
            rounded = kept([P, PASSES, P, PACK], BF16, "w_rounded%d_%d" % (w, b), tag=tag)
            parts = [slice(a, a + 1) for a in range(PASSES)] if b == 0 else [slice(0, PASSES)]
            for part in parts:
                nc.scalar.copy(
                    out=rounded[:, part].rearrange("p a (c i) j -> p a c j i", i=LINE),
                    in_=raws[w, b][:, part].rearrange("p a j (c i) -> p a c j i", i=LINE),
                )
            w_codes[w, b] = kept([P, PASSES, P], U32, "w_codes%d_%d" % (w, b))
            w_scales[w, b] = kept([P, PASSES, P], U8, "w_scales%d_%d" % (w, b))
            nc.vector.quantize_mx(
                out=w_codes[w, b][:].rearrange("p a c -> p (a c)").bitcast(FP8X4),
                scales=w_scales[w, b][:].rearrange("p a c -> p (a c)"),
                in_=rounded[:].rearrange("p a c j -> p (a c j)"),
            )

        gather_words(0, 0)
        nc.vector.tensor_copy(got_s[:], tab_s[:].indirect(idx1[:]))
        for q in range(QUADS):
            nc.sync.dma_start(
                out=got_s1[scale_partitions(q), :].bitcast(I32),
                in_=got_s[QUAD * q + SCALE_ROWS : QUAD * q + 2 * SCALE_ROWS, :].bitcast(I32),
            )
        gather_words(1, 0)
        quantise_weight(0, 0)
        quantise_weight(1, 0)
        gather_words(1, 1, tag=first_tag(-1))
        gather_words(0, 1, tag=prod_tag(-1))

        nc.sync.dma_start(idx2[:], offs2)
        nc.sync.dma_start(idx3[:], offs3)
        nc.sync.dma_start(out=wgs_t[0][:], in_=wgs[:, 0:HALF])
        load_page(0)
        load_weights(1)
        nc.sync.dma_start(out=wgs_t[1][:], in_=wgs[:, HALF:S])
        with nc.allow_non_contiguous_dma(reason="one gain for each row of a block, rows on the partitions"):
            nc.sync.dma_start(out=gain_t[:], in_=gain.rearrange("(b p) -> p b", p=P))
        load_weights(2)
        load_page(1)
        load_weights(3)
        load_page(2)
        load_page(3)
        nc.sync.dma_start(out=w5_raw[:], in_=w5.rearrange("(p j) c -> p j c", j=PACK))
        nc.sync.dma_start(out=w4_raw[:], in_=w4_words[0].rearrange("p c i -> p (c i)").bitcast(I32))
        for q in range(QUADS):
            nc.sync.dma_start(
                out=w4_s_raw[scale_partitions(q), :].bitcast(I32),
                in_=w4_scales[0, scale_rows(q), :].bitcast(I32),
            )

        def products(b, h):
            cols = slice(HALF * h, HALF * (h + 1))
            first, second, third = [
                psum.tile([P, HALF], F32, name="sum%d_%d_%d" % (b, h, i), tag="bank%d" % (3 * h + i))[:]
                for i in range(3)
            ]

            def multiply_by_weight(w, bank):
                for a in range(PASSES):
                    nc.tensor.matmul_mx(
                        out=bank,
                        lhsT=w_codes[w, b][:, a, :].bitcast(FP8X4),
                        lhsT_scale=w_scales[w, b][:, a, :],
                        rhs=got_w[a, h][:].bitcast(FP8X4),
                        rhs_scale=got_s[SCALE_ROWS * a : P, cols],
                        start=(a == 0),
                        stop=(a == PASSES - 1),
                    )

            multiply_by_weight(0, first)
            for a in range(PASSES):
                nc.tensor.matmul_mx(
                    out=second,
                    lhsT=w2_w[:, a, 2 * P * b : 2 * P * (b + 1)].bitcast(FP4X4),
                    lhsT_scale=w2_s[:, a, P * b : P * (b + 1)],
                    rhs=got_w[a, h][:].bitcast(FP8X4),
                    rhs_scale=(got_s, got_s1)[a][:, cols],
                    start=(a == 0),
                    stop=(a == PASSES - 1),
                )
            multiply_by_weight(1, third)
            first_sb = kept([P, HALF], F32, "first_sb%d_%d" % (b, h), tag=first_tag(2 * b + h))
            nc.scalar.copy(out=first_sb[:], in_=first)
            follows_next_weights = h == HALVES - 1 and 0 < b < BLOCKS - 1
            prod = kept([P, HALF], F32, "prod%d_%d" % (b, h), tag=prod_tag(b if follows_next_weights else 2 * b + h))
            nc.vector.tensor_tensor(prod[:], second, first_sb[:], ALU.mult)
            return prod, third, first_sb

        def put(b, h, h_sb):
            nc.vector.tensor_tensor(pages[b][:].indirect(half_of(idx2, h)), h_sb[:], wgs_t[h][:], ALU.mult)

        z_rows = [kept([P, PACK, HALF], BF16, "z_rows%d" % h) for h in range(HALVES)]

        def look(b, neg_top):
            nc.vector.tensor_reduce(neg_top, pages[b][:], AXIS.X, ALU.max, negate=True)
            for h in range(HALVES):
                a_sb = ring.tile([P, HALF], F32, name="a_sb")
                nc.scalar.activation(
                    out=a_sb[:], in_=pages[b][:].indirect(half_of(idx3, h)), func=ACT.Exp, bias=neg_top
                )
                z_sb = ring.tile([P, HALF], BF16, name="z_sb")
                if b == BLOCKS - 1:
                    nc.vector.tensor_scalar(z_sb[:], a_sb[:], gain_t[:, b : b + 1], None, ALU.mult)
                else:
                    nc.scalar.activation(out=z_sb[:], in_=a_sb[:], func=ACT.Copy, scale=gain_t[:, b : b + 1])
                for t in range(PACK):
                    nc.sync.dma_start(out=z_rows[h][QUAD * b : QUAD * (b + 1), t, :], in_=z_sb[t:P:PACK, :])

        prod, third = products(0, 0)[:2]
        h_first = kept([P, HALF], F32, "h_first")
        nc.vector.tensor_tensor(h_first[:], third, prod[:], ALU.add)
        prod, third = products(0, 1)[:2]
        put(0, 0, h_first)
        quantise_weight(0, 1)
        quantise_weight(1, 1)
        h_second = kept([P, HALF], F32, "h_second", tag=prod_tag(0))
        nc.vector.tensor_tensor(h_second[:], third, prod[:], ALU.add)
        put(0, 1, h_second)

        for b in range(1, BLOCKS):
            if b + 1 < BLOCKS:
                quantise_weight(0, b + 1)
                quantise_weight(1, b + 1)
            both = [products(b, h) for h in range(HALVES)]
            h_sb = [kept([P, HALF], F32, "h_sb%d_%d" % (b, h), tag="h_sb%d" % h) for h in range(HALVES)]
            for h in range(HALVES):
                prod, third = both[h][:2]
                third_sb = ring.tile([P, HALF], F32, name="third_sb")
                nc.scalar.copy(out=third_sb[:], in_=third)
                nc.gpsimd.tensor_tensor(h_sb[h][:], third_sb[:], prod[:], ALU.add)
            look(b - 1, both[HALVES - 1][2][:, 0:1])
            for h in range(HALVES):
                put(b, h, h_sb[h])
        last_top = kept([P, 1], F32, "last_top")
        look(BLOCKS - 1, last_top[:])

        w4_w = kept([P, PACK, P], I32, "w4_w", tag=first_tag(2 * (BLOCKS - 2)))
        w4_s = kept([P, PACK, P], U8, "w4_s", tag="wgs_t1")
        nc.scalar.copy(out=w4_w[:].bitcast(U32), in_=w4_raw[:].bitcast(U32).rearrange("p (m t) -> p t m", t=PACK))
        nc.vector.tensor_copy(out=w4_s[:], in_=w4_s_raw[:].rearrange("p (m t) -> p t m", t=PACK))
        w5_rounded = kept([P, PACK, P, PACK], BF16, "w5_rounded", tag=prod_tag(2 * (BLOCKS - 1)))
        nc.scalar.copy(out=w5_rounded[:], in_=w5_raw[:].rearrange("p j (m t) -> p t m j", t=PACK))
        w5_w = kept([P, PACK, P], U32, "w5_w", tag="h_sb1")
        w5_s = kept([P, PACK, P], U8, "w5_s")
        nc.vector.quantize_mx(
            out=w5_w[:].rearrange("p t m -> p (t m)").bitcast(FP8X4),
            scales=w5_s[:].rearrange("p t m -> p (t m)"),
            in_=w5_rounded[:].rearrange("p t m j -> p (t m j)"),
        )

        y_words = kept([P, M], I32, "y_words")
        y_scales = kept([P, M], U8, "y_scales")
        out_rows = out_0.rearrange("(p t) m -> p t m", t=PACK)
        out_words = out_1[0].rearrange("p m t -> p (m t)").bitcast(I32)

        def interleave(on_scalar, out, rows):
            copy = nc.scalar.copy if on_scalar else nc.vector.tensor_copy
            copy(
                out=out.rearrange("p (c i) t -> p c t i", i=LINE),
                in_=rows.rearrange("p t (c i) -> p c t i", i=LINE),
            )

        def quantise_z(c):
            h, lo = divmod(CHUNK * c, HALF)
            z_in = kept([P, CHUNK, PACK], BF16, "z_in%d" % c)
            interleave(c in SCALAR_Z_CHUNKS, z_in[:], z_rows[h][:, :, lo : lo + CHUNK])
            z_w = kept([P, CHUNK], U32, "z_w%d" % c)
            z_s = kept([P, CHUNK], U8, "z_s%d" % c)
            nc.vector.quantize_mx(out=z_w[:].bitcast(FP8X4), scales=z_s[:], in_=z_in[:].rearrange("p m t -> p (m t)"))
            return z_w, z_s

        def second_stage(c, z_w, z_s):
            y = kept([P, PACK, CHUNK], F32, "y%d" % c)
            for pair in range(PACK // 2):
                at = 4 * (c % 2) + 2 * pair
                plain = psum.tile([P, 2, CHUNK], F32, name="plain%d_%d" % (c, pair), tag="bank%d" % at)
                other = psum.tile([P, 2, CHUNK], F32, name="other%d_%d" % (c, pair), tag="bank%d" % (at + 1))
                for codes, scales, bank in ((w5_w, w5_s, other), (w4_w, w4_s, plain)):
                    for i in range(2):
                        t = 2 * pair + i
                        nc.tensor.matmul_mx(
                            out=bank[:, i, :],
                            lhsT=codes[:, t, :].bitcast(FP8X4),
                            lhsT_scale=scales[:, t, :],
                            rhs=z_w[:].bitcast(FP8X4),
                            rhs_scale=z_s[:],
                            start=True,
                            stop=True,
                        )
                size = ring.tile([P, 2, CHUNK], F32, name="size")
                nc.scalar.activation(out=size[:], in_=other[:], func=ACT.Abs)
                nc.vector.tensor_tensor(y[:, 2 * pair : 2 * pair + 2, :], plain[:], size[:], ALU.add)
            cols = slice(CHUNK * c, CHUNK * (c + 1))
            nc.sync.dma_start(out=out_rows[:, :, cols], in_=y[:])
            return y

        def planes(c, y):
            cols = slice(CHUNK * c, CHUNK * (c + 1))
            y_in = ring.tile([P, CHUNK, PACK], BF16, name="y_in", align_bytes=64)
            interleave(c in SCALAR_Y_CHUNKS, y_in[:], y[:])
            nc.vector.quantize_mx(
                out=y_words[:, cols].bitcast(FP8X4), scales=y_scales[:, cols], in_=y_in[:].rearrange("p m t -> p (m t)")
            )
            nc.sync.dma_start(out=out_words[:, cols], in_=y_words[:, cols])

        zq = [quantise_z(0), quantise_z(1)]
        ys = []
        for c in range(CHUNKS):
            ys.append(second_stage(c, *zq[c]))
            if c + 2 < CHUNKS:
                zq.append(quantise_z(c + 2))
            if c > 0:
                planes(c - 1, ys[c - 1])
        planes(CHUNKS - 1, ys[CHUNKS - 1])
        for q in range(QUADS):
            nc.scalar.dma_start(
                out=out_2[0, scale_rows(q), :].bitcast(I32), in_=y_scales[scale_partitions(q), :].bitcast(I32)
            )
